import numpy as np
import ml_dtypes


def mxq(x, axis, fmt="e4m3"):
    dtype, down = {"e4m3": (ml_dtypes.float8_e4m3fn, 7), "e5m2": (ml_dtypes.float8_e5m2, 14)}[fmt]
    v = np.moveaxis(np.asarray(x, np.float32).astype(ml_dtypes.bfloat16).astype(np.float64), axis, -1)
    blocks = v.reshape(v.shape[:-1] + (-1, 32))
    amax = np.abs(blocks).max(-1, keepdims=True)
    byte = np.maximum(np.where(amax > 0, np.frexp(amax)[1] - 1 + 127, 0) - down, 1)
    scale = np.exp2(byte - 127.0)
    codes = (blocks / scale).astype(np.float32).astype(dtype).astype(np.float64)
    return np.moveaxis((codes * scale).reshape(v.shape), -1, axis)


WIDE = False


def mx_kscale(k):
    if not WIDE:
        return np.ones(k)
    levels = np.array([10, -10, 5, -5, 0])
    if k % 512:
        return np.exp2(np.random.permutation(np.resize(levels, k // 32))).repeat(32)
    a = np.empty((k // 512, 16))
    for p in range(k // 512):
        a[p, :8] = np.random.permutation(np.resize(levels, 8))
        for g in range(8):
            far = levels[np.abs(levels - a[p, g]) >= 10]
            a[p, g + 8] = far[np.random.randint(len(far))]
    return np.exp2(a.ravel()).repeat(32)


def f64(x):
    return np.asarray(x).astype(np.float64)


def striped(idx):
    return np.tile(np.asarray(idx).reshape(-1, 16).T, (8, 1)).astype(np.uint16)


def unstriped(offs):
    return offs[:16].T.reshape(-1).astype(np.int64)


B, N, T, D, DV, NQ = 1, 512, 1024, 512, 256, 128
SINKS = 64


def setup_inputs():
    n = np.random.standard_normal
    head = np.random.randint(0, T // B)
    ring = T // B
    sinks = np.arange(SINKS)
    win = SINKS + (head + np.arange(N - SINKS)) % (ring - SINKS)
    idx = np.concatenate([b * ring + np.concatenate([sinks, win]) for b in range(B)])
    s = mx_kscale(D)[:, None]
    u = np.ones(T)
    u[idx] = mx_kscale(B * N)
    r = np.random.uniform(0.5, 2.0, T)
    k = n((D, T)) / s
    v = n((DV, T)) / (u * r)
    when = np.zeros(T)
    when[idx] = np.sort(np.random.permutation(2 * N)[:B * N])
    return {
        "qT": (n((B, D, NQ)) * s * (0.60 / np.sqrt(D))).astype(np.float32),
        "kT": k.astype(np.float32),
        "vT": v.astype(np.float32),
        "vs": np.tile(u * r, (128, 1)).astype(np.float32),
        "pos": np.tile(when, (128, 1)).astype(np.float32),
        "slope": np.exp2(-np.random.randint(8, 13, (B, NQ, 1))).astype(np.float32),
        "offs": striped(idx),
    }


def reference(qT, kT, vT, vs, pos, slope, offs):
    idx = unstriped(offs)
    k = f64(kT)
    v = f64(vT)
    pick = lambda x: x[:, idx].reshape(x.shape[0], B, N).transpose(1, 0, 2)
    q = f64(qT)
    score = mxq(q, 1, "e4m3").transpose(0, 2, 1) @ mxq(pick(k), 1, "e4m3")
    score = score + f64(slope) * pick(f64(pos))[:, :1, :]
    m = score.max(-1, keepdims=True)
    p = np.exp(score - m)
    total = p.sum(-1, keepdims=True)
    w = p * pick(f64(vs))[:, :1, :]
    y = mxq(w, 2, "e4m3") @ mxq(pick(v).transpose(0, 2, 1), 1, "e4m3")
    y = y / total
    return y

@@ -1,0 +1,160 @@
+from contextlib import ExitStack
+
+import concourse.mybir as mybir
+from concourse.masks import make_identity
+
+NQ, D, N, T, DV = 128, 512, 512, 1024, 256
+P = 128
+FLOPS = 2 * NQ * N * (D + DV)
+
+F32 = mybir.dt.float32
+BF16 = mybir.dt.bfloat16
+U32 = mybir.dt.uint32
+U16 = mybir.dt.uint16
+U8 = mybir.dt.uint8
+FP8X4 = mybir.dt.float8_e4m3fn_x4
+ADD, MULT, MAX = mybir.AluOpType.add, mybir.AluOpType.mult, mybir.AluOpType.max
+EXP = mybir.ActivationFunctionType.Exp
+COPY = mybir.ActivationFunctionType.Copy
+X = mybir.AxisListType.X
+
+
+def tile_attend_ring_alibi_kernel(tc, qT, kT, vT, vs, pos, slope, offs, out):
+    nc = tc.nc
+    with ExitStack() as ctx:
+        held = ctx.enter_context(tc.tile_pool(name="held", bufs=1))
+        psum = ctx.enter_context(tc.psum_pool(name="psum", bufs=1))
+
+        offsets = held.tile([P, N // 16], U16, name="offsets")
+        k_raw = [held.tile([P, 2, T], F32, name=f"k_raw{u}") for u in range(2)]
+        k_pairs = [held.tile([P, 2 * T], BF16, name=f"k_pairs{u}", align_bytes=64) for u in range(2)]
+        v_raw = held.tile([P, 2, T], F32, name="v_raw")
+        v_pairs = held.tile([P, 2 * T], BF16, name="v_pairs", align_bytes=64)
+        q_raw = held.tile([P, 4, NQ], F32, name="q_raw")
+        pos_pool = held.tile([P, T], F32, name="pos_pool")
+        vs_pool = held.tile([P, T], F32, name="vs_pool")
+        slope_col = held.tile([P, 1], F32, name="slope_col")
+
+        k_rows = kT.rearrange("(p t) n -> p t n", t=4)
+        v_rows = vT.rearrange("(p t) n -> p t n", t=2)
+
+        def load_half(tile, rows, h, parts=2):
+            cols = slice(h * (T // parts), (h + 1) * (T // parts))
+            nc.sync.dma_start(out=tile[:, :, cols], in_=rows[:, :, cols])
+
+        load_half(k_raw[0], k_rows[:, 0:2, :], 0)
+        nc.sync.dma_start(offsets[:], offs)
+        load_half(k_raw[0], k_rows[:, 0:2, :], 1)
+        nc.sync.dma_start(out=q_raw[:], in_=qT[0].rearrange("(p t) q -> p t q", t=4))
+        load_half(k_raw[1], k_rows[:, 2:4, :], 0)
+        load_half(k_raw[1], k_rows[:, 2:4, :], 1)
+        nc.sync.dma_start(out=pos_pool[:], in_=pos)
+        nc.sync.dma_start(out=slope_col[:], in_=slope[0])
+        load_half(v_raw, v_rows, 0)
+        load_half(v_raw, v_rows, 1)
+        nc.sync.dma_start(out=vs_pool[:], in_=vs)
+
+        warm = held.tile([P, 1], F32, name="warm")
+        warm_out = held.tile([P, 1], F32, name="warm_out")
+        nc.vector.memset(warm[:], 0.0)
+        nc.scalar.activation(warm_out[:], warm[:], EXP)
+        ident = held.tile([P, P], F32, name="ident")
+        make_identity(nc, ident[:])
+
+        def pair_up(engine, pairs, raw, a, b):
+            dst = pairs[:, 2 * a : 2 * b].rearrange("p (n t) -> p n t", t=2)
+            src = raw[:, :, a:b].rearrange("p t n -> p n t")
+            if engine == "scalar":
+                nc.scalar.activation(dst, src, COPY)
+            else:
+                nc.vector.tensor_copy(out=dst, in_=src)
+
+        def quantise(name, src, width):
+            codes = held.tile([P, width], U32, name=name + "_codes", align_bytes=64)
+            scales = held.tile([P, width], U8, name=name + "_scales", align_bytes=64)
+            return codes, scales
+
+        k_words = held.tile([P, N, 2], U32, name="k_words", align_bytes=64)
+        pair_up("scalar", k_pairs[0], k_raw[0], 0, 512)
+        pair_up("scalar", k_pairs[0], k_raw[0], 512, 1024)
+        q_grouped = held.tile([P, NQ, 4], BF16, name="q_grouped", align_bytes=64)
+        nc.vector.tensor_copy(out=q_grouped[:], in_=q_raw[:].rearrange("p t q -> p q t"))
+        nc.vector.tensor_copy(k_words[:, :, 0], k_pairs[0][:].bitcast(U32).indirect(offsets[:]))
+        q_codes, q_scales = quantise("q", None, NQ)
+        nc.vector.quantize_mx(out=q_codes[:].bitcast(FP8X4), scales=q_scales[:], in_=q_grouped[:].rearrange("p q t -> p (q t)"))
+        pair_up("scalar", k_pairs[1], k_raw[1], 0, 512)
+        pair_up("scalar", k_pairs[1], k_raw[1], 512, 688)
+        pair_up("vector", k_pairs[1], k_raw[1], 688, 1024)
+        nc.vector.tensor_copy(k_words[:, :, 1], k_pairs[1][:].bitcast(U32).indirect(offsets[:]))
+        k_codes, k_scales = quantise("k", None, N)
+        k_flat = k_words[:].rearrange("p n u -> p (n u)").bitcast(BF16)
+        H = N // 2
+        scores = []
+        for h in range(2):
+            cols = slice(h * H, (h + 1) * H)
+            nc.vector.quantize_mx(out=k_codes[:, cols].bitcast(FP8X4), scales=k_scales[:, cols], in_=k_flat[:, 4 * h * H : 4 * (h + 1) * H])
+            bank = psum.tile([P, H], F32, name=f"scores{h}")
+            nc.tensor.matmul_mx(out=bank[:], lhsT=q_codes[:].bitcast(FP8X4), lhsT_scale=q_scales[:], rhs=k_codes[:, cols].bitcast(FP8X4), rhs_scale=k_scales[:, cols], start=True, stop=True)
+            scores.append(bank)
+
+        pair_up("scalar", v_pairs, v_raw, 0, 512)
+        pos_listed = held.tile([P, N], F32, name="pos_listed")
+        nc.vector.tensor_copy(pos_listed[:], pos_pool[:].indirect(offsets[:]))
+        s = held.tile([P, N], F32, name="s")
+        for h in range(2):
+            cols = slice(h * H, (h + 1) * H)
+            nc.vector.scalar_tensor_tensor(out=s[:, cols], in0=pos_listed[:, cols], scalar=slope_col[:], in1=scores[h][:], op0=MULT, op1=ADD)
+        minus_m = held.tile([P, 1], F32, name="minus_m")
+        nc.vector.tensor_reduce(out=minus_m[:], in_=s[:], axis=X, op=MAX, negate=True)
+
+        pair_up("vector", v_pairs, v_raw, 512, 1024)
+        s4 = s[:].rearrange("p (i u e) -> p i u e", u=2, e=2)
+        pr, sums = [], []
+        for u in range(2):
+            pu = held.tile([P, N // 4, 2], F32, name=f"p{u}")
+            su = held.tile([P, 1], F32, name=f"sum{u}")
+            nc.scalar.activation(pu[:], s4[:, :, u, :], EXP, bias=minus_m[:], accum_out=su[:])
+            pr.append(pu)
+            sums.append(su)
+
+        v_words = held.tile([P, N], U32, name="v_words", align_bytes=64)
+        nc.vector.tensor_copy(v_words[:], v_pairs[:].bitcast(U32).indirect(offsets[:]))
+        v_bank = psum.tile([P, 4, P], F32, name="v_bank")
+        v_f32 = v_words[:].bitcast(F32)
+        for t in range(4):
+            nc.tensor.transpose(v_bank[:, t, :], v_f32[:, t : N : 4], ident[:])
+        v_grouped = held.tile([P, DV, 4], BF16, name="v_grouped", align_bytes=64)
+        v_turned = v_bank[:].rearrange("p t w -> p (t w)").bitcast(BF16).rearrange("p (t e) -> p e t", t=4)
+        nc.scalar.copy(v_grouped[:], v_turned)
+        v_codes, v_scales = quantise("v", None, DV)
+
+        vs_listed = held.tile([P, N], F32, name="vs_listed")
+        nc.vector.tensor_copy(vs_listed[:], vs_pool[:].indirect(offsets[:]))
+        vs4 = vs_listed[:].rearrange("p (i u e) -> p i u e", u=2, e=2)
+        w_bank = psum.tile([P, 2, P], F32, name="w_bank")
+        for u in range(2):
+            wu = held.tile([P, N // 4, 2], BF16, name=f"w{u}", align_bytes=64)
+            nc.vector.tensor_tensor(wu[:], pr[u][:], vs4[:, :, u, :], MULT)
+            nc.tensor.transpose(w_bank[:, u, :], wu[:].rearrange("p i e -> p (i e)").bitcast(F32), ident[:])
+        w_grouped = held.tile([P, NQ, 4], BF16, name="w_grouped", align_bytes=64)
+        w_words = w_grouped[:].rearrange("p q t -> p (q t)").bitcast(F32).rearrange("p (q u) -> p q u", u=2)
+        nc.vector.tensor_copy(out=w_words, in_=w_bank[:].rearrange("p u q -> p q u"))
+        total = held.tile([P, 1], F32, name="total")
+        nc.vector.tensor_tensor(total[:], sums[0][:], sums[1][:], ADD)
+        inv = held.tile([P, 1], F32, name="inv")
+        nc.vector.reciprocal(inv[:], total[:])
+        nc.vector.quantize_mx(out=v_codes[:].bitcast(FP8X4), scales=v_scales[:], in_=v_grouped[:].rearrange("p e t -> p (e t)"))
+        w_codes, w_scales = quantise("w", None, NQ)
+        nc.vector.quantize_mx(out=w_codes[:].bitcast(FP8X4), scales=w_scales[:], in_=w_grouped[:].rearrange("p q t -> p (q t)"))
+
+        HV = DV // 2
+        for h in range(2):
+            cols = slice(h * HV, (h + 1) * HV)
+            y = psum.tile([P, HV], F32, name=f"y{h}")
+            nc.tensor.matmul_mx(out=y[:], lhsT=w_codes[:].bitcast(FP8X4), lhsT_scale=w_scales[:], rhs=v_codes[:, cols].bitcast(FP8X4), rhs_scale=v_scales[:, cols], start=True, stop=True)
+            res = held.tile([P, HV], F32, name=f"res{h}")
+            if h == 0:
+                nc.scalar.activation(res[:], y[:], COPY, scale=inv[:])
+            else:
+                nc.vector.tensor_scalar(res[:], y[:], inv[:], None, MULT)
+            nc.sync.dma_start(out=out[0][:, cols], in_=res[:])

@@ -31,6 +31,8 @@ def tile_attend_ring_alibi_kernel(tc, qT, kT, vT, vs, pos, slope, offs, out):
         v_raw = held.tile([P, 2, T], F32, name="v_raw")
         v_pairs = held.tile([P, 2 * T], BF16, name="v_pairs", align_bytes=64)
         q_raw = held.tile([P, 4, NQ], F32, name="q_raw")
+        pos_cols = held.tile([P, 8], F32, name="pos_cols")
+        vs_cols = held.tile([P, 8], F32, name="vs_cols")
         pos_pool = held.tile([P, T], F32, name="pos_pool")
         vs_pool = held.tile([P, T], F32, name="vs_pool")
         slope_col = held.tile([P, 1], F32, name="slope_col")
@@ -42,17 +44,17 @@ def tile_attend_ring_alibi_kernel(tc, qT, kT, vT, vs, pos, slope, offs, out):
             cols = slice(h * (T // parts), (h + 1) * (T // parts))
             nc.sync.dma_start(out=tile[:, :, cols], in_=rows[:, :, cols])
 
+        nc.sync.dma_start(out=pos_cols[:], in_=pos[0].rearrange("(p j) -> p j", j=8))
+        nc.sync.dma_start(out=vs_cols[:], in_=vs[0].rearrange("(p j) -> p j", j=8))
         load_half(k_raw[0], k_rows[:, 0:2, :], 0)
         nc.sync.dma_start(offsets[:], offs)
         load_half(k_raw[0], k_rows[:, 0:2, :], 1)
-        nc.sync.dma_start(out=q_raw[:], in_=qT[0].rearrange("(p t) q -> p t q", t=4))
         load_half(k_raw[1], k_rows[:, 2:4, :], 0)
         load_half(k_raw[1], k_rows[:, 2:4, :], 1)
-        nc.sync.dma_start(out=pos_pool[:], in_=pos)
+        nc.sync.dma_start(out=q_raw[:], in_=qT[0].rearrange("(p t) q -> p t q", t=4))
         nc.sync.dma_start(out=slope_col[:], in_=slope[0])
         load_half(v_raw, v_rows, 0)
         load_half(v_raw, v_rows, 1)
-        nc.sync.dma_start(out=vs_pool[:], in_=vs)
 
         warm = held.tile([P, 1], F32, name="warm")
         warm_out = held.tile([P, 1], F32, name="warm_out")
@@ -74,18 +76,31 @@ def tile_attend_ring_alibi_kernel(tc, qT, kT, vT, vs, pos, slope, offs, out):
             scales = held.tile([P, width], U8, name=name + "_scales", align_bytes=64)
             return codes, scales
 
+        def spread(cols, pool, copy, tag):
+            for b in range(2):
+                bank = psum.tile([P, 4, P], F32, name=f"{tag}{b}", tag=f"{tag}{b}")
+                for j in range(4):
+                    nc.tensor.transpose(bank[:, j, :], cols[:, 4 * b + j : 4 * b + j + 1].to_broadcast([P, P]), ident[:])
+                copy(pool[:].rearrange("p (n j) -> p n j", j=8)[:, :, 4 * b : 4 * b + 4], bank[:].rearrange("p j n -> p n j"))
+
+        spread(pos_cols, pos_pool, lambda o, i: nc.vector.tensor_copy(out=o, in_=i), "spread_a")
         k_words = held.tile([P, N, 2], U32, name="k_words", align_bytes=64)
         pair_up("scalar", k_pairs[0], k_raw[0], 0, 512)
-        pair_up("scalar", k_pairs[0], k_raw[0], 512, 1024)
-        q_grouped = held.tile([P, NQ, 4], BF16, name="q_grouped", align_bytes=64)
-        nc.vector.tensor_copy(out=q_grouped[:], in_=q_raw[:].rearrange("p t q -> p q t"))
+        pair_up("vector", k_pairs[0], k_raw[0], 512, 1024)
         nc.vector.tensor_copy(k_words[:, :, 0], k_pairs[0][:].bitcast(U32).indirect(offsets[:]))
-        q_codes, q_scales = quantise("q", None, NQ)
-        nc.vector.quantize_mx(out=q_codes[:].bitcast(FP8X4), scales=q_scales[:], in_=q_grouped[:].rearrange("p q t -> p (q t)"))
+        spread(vs_cols, vs_pool, lambda o, i: nc.scalar.activation(o, i, COPY), "spread_b")
+        pos_listed = held.tile([P, N], F32, name="pos_listed")
+        nc.vector.tensor_copy(pos_listed[:], pos_pool[:].indirect(offsets[:]))
+        vs_listed = held.tile([P, N], F32, name="vs_listed")
+        nc.vector.tensor_copy(vs_listed[:], vs_pool[:].indirect(offsets[:]))
         pair_up("scalar", k_pairs[1], k_raw[1], 0, 512)
         pair_up("scalar", k_pairs[1], k_raw[1], 512, 688)
         pair_up("vector", k_pairs[1], k_raw[1], 688, 1024)
         nc.vector.tensor_copy(k_words[:, :, 1], k_pairs[1][:].bitcast(U32).indirect(offsets[:]))
+        q_grouped = held.tile([P, NQ, 4], BF16, name="q_grouped", align_bytes=64)
+        nc.scalar.activation(q_grouped[:], q_raw[:].rearrange("p t q -> p q t"), COPY)
+        q_codes, q_scales = quantise("q", None, NQ)
+        nc.vector.quantize_mx(out=q_codes[:].bitcast(FP8X4), scales=q_scales[:], in_=q_grouped[:].rearrange("p q t -> p (q t)"))
         k_codes, k_scales = quantise("k", None, N)
         k_flat = k_words[:].rearrange("p n u -> p (n u)").bitcast(BF16)
         H = N // 2
@@ -98,8 +113,7 @@ def tile_attend_ring_alibi_kernel(tc, qT, kT, vT, vs, pos, slope, offs, out):
             scores.append(bank)
 
         pair_up("scalar", v_pairs, v_raw, 0, 512)
-        pos_listed = held.tile([P, N], F32, name="pos_listed")
-        nc.vector.tensor_copy(pos_listed[:], pos_pool[:].indirect(offsets[:]))
+        pair_up("scalar", v_pairs, v_raw, 512, 768)
         s = held.tile([P, N], F32, name="s")
         for h in range(2):
             cols = slice(h * H, (h + 1) * H)
@@ -107,7 +121,7 @@ def tile_attend_ring_alibi_kernel(tc, qT, kT, vT, vs, pos, slope, offs, out):
         minus_m = held.tile([P, 1], F32, name="minus_m")
         nc.vector.tensor_reduce(out=minus_m[:], in_=s[:], axis=X, op=MAX, negate=True)
 
-        pair_up("vector", v_pairs, v_raw, 512, 1024)
+        pair_up("vector", v_pairs, v_raw, 768, 1024)
         s4 = s[:].rearrange("p (i u e) -> p i u e", u=2, e=2)
         pr, sums = [], []
         for u in range(2):
@@ -128,8 +142,6 @@ def tile_attend_ring_alibi_kernel(tc, qT, kT, vT, vs, pos, slope, offs, out):
         nc.scalar.copy(v_grouped[:], v_turned)
         v_codes, v_scales = quantise("v", None, DV)
 
-        vs_listed = held.tile([P, N], F32, name="vs_listed")
-        nc.vector.tensor_copy(vs_listed[:], vs_pool[:].indirect(offsets[:]))
         vs4 = vs_listed[:].rearrange("p (i u e) -> p i u e", u=2, e=2)
         w_bank = psum.tile([P, 2, P], F32, name="w_bank")
         for u in range(2):
@@ -138,7 +150,7 @@ def tile_attend_ring_alibi_kernel(tc, qT, kT, vT, vs, pos, slope, offs, out):
             nc.tensor.transpose(w_bank[:, u, :], wu[:].rearrange("p i e -> p (i e)").bitcast(F32), ident[:])
         w_grouped = held.tile([P, NQ, 4], BF16, name="w_grouped", align_bytes=64)
         w_words = w_grouped[:].rearrange("p q t -> p (q t)").bitcast(F32).rearrange("p (q u) -> p q u", u=2)
-        nc.vector.tensor_copy(out=w_words, in_=w_bank[:].rearrange("p u q -> p q u"))
+        nc.scalar.copy(w_words, w_bank[:].rearrange("p u q -> p q u"))
         total = held.tile([P, 1], F32, name="total")
         nc.vector.tensor_tensor(total[:], sums[0][:], sums[1][:], ADD)
         inv = held.tile([P, 1], F32, name="inv")
@@ -150,7 +162,7 @@ def tile_attend_ring_alibi_kernel(tc, qT, kT, vT, vs, pos, slope, offs, out):
         HV = DV // 2
         for h in range(2):
             cols = slice(h * HV, (h + 1) * HV)
-            y = psum.tile([P, HV], F32, name=f"y{h}")
+            y = psum.tile([P, HV], F32, name=f"y{h}", tag=f"spread_a{h}")
             nc.tensor.matmul_mx(out=y[:], lhsT=w_codes[:].bitcast(FP8X4), lhsT_scale=w_scales[:], rhs=v_codes[:, cols].bitcast(FP8X4), rhs_scale=v_scales[:, cols], start=True, stop=True)
             res = held.tile([P, HV], F32, name=f"res{h}")
             if h == 0:

@@ -28,11 +28,9 @@ def tile_attend_ring_alibi_kernel(tc, qT, kT, vT, vs, pos, slope, offs, out):
         offsets = held.tile([P, N // 16], U16, name="offsets")
         k_raw = [held.tile([P, 2, T], F32, name=f"k_raw{u}") for u in range(2)]
         k_pairs = [held.tile([P, 2 * T], BF16, name=f"k_pairs{u}", align_bytes=64) for u in range(2)]
-        v_raw = held.tile([P, 2, T], F32, name="v_raw")
-        v_pairs = held.tile([P, 2 * T], BF16, name="v_pairs", align_bytes=64)
+        v_raw = [held.tile([P, 2, T // 2], F32, name=f"v_raw{h}", tag=f"v_raw{h}") for h in range(2)]
+        v_pairs = held.tile([P, 2 * T], BF16, name="v_pairs", tag="v_pairs", align_bytes=64)
         q_raw = held.tile([P, 4, NQ], F32, name="q_raw")
-        pos_cols = held.tile([P, 8], F32, name="pos_cols")
-        vs_cols = held.tile([P, 8], F32, name="vs_cols")
         pos_pool = held.tile([P, T], F32, name="pos_pool")
         vs_pool = held.tile([P, T], F32, name="vs_pool")
         slope_col = held.tile([P, 1], F32, name="slope_col")
@@ -44,17 +42,17 @@ def tile_attend_ring_alibi_kernel(tc, qT, kT, vT, vs, pos, slope, offs, out):
             cols = slice(h * (T // parts), (h + 1) * (T // parts))
             nc.sync.dma_start(out=tile[:, :, cols], in_=rows[:, :, cols])
 
-        nc.sync.dma_start(out=pos_cols[:], in_=pos[0].rearrange("(p j) -> p j", j=8))
-        nc.sync.dma_start(out=vs_cols[:], in_=vs[0].rearrange("(p j) -> p j", j=8))
         load_half(k_raw[0], k_rows[:, 0:2, :], 0)
         nc.sync.dma_start(offsets[:], offs)
         load_half(k_raw[0], k_rows[:, 0:2, :], 1)
+        nc.sync.dma_start(out=pos_pool[:], in_=pos)
         load_half(k_raw[1], k_rows[:, 2:4, :], 0)
         load_half(k_raw[1], k_rows[:, 2:4, :], 1)
         nc.sync.dma_start(out=q_raw[:], in_=qT[0].rearrange("(p t) q -> p t q", t=4))
         nc.sync.dma_start(out=slope_col[:], in_=slope[0])
-        load_half(v_raw, v_rows, 0)
-        load_half(v_raw, v_rows, 1)
+        for h in range(2):
+            nc.sync.dma_start(out=v_raw[h][:], in_=v_rows[:, :, h * (T // 2) : (h + 1) * (T // 2)])
+        nc.sync.dma_start(out=vs_pool[:], in_=vs)
 
         warm = held.tile([P, 1], F32, name="warm")
         warm_out = held.tile([P, 1], F32, name="warm_out")
@@ -76,26 +74,15 @@ def tile_attend_ring_alibi_kernel(tc, qT, kT, vT, vs, pos, slope, offs, out):
             scales = held.tile([P, width], U8, name=name + "_scales", align_bytes=64)
             return codes, scales
 
-        def spread(cols, pool, copy, tag):
-            for b in range(2):
-                bank = psum.tile([P, 4, P], F32, name=f"{tag}{b}", tag=f"{tag}{b}")
-                for j in range(4):
-                    nc.tensor.transpose(bank[:, j, :], cols[:, 4 * b + j : 4 * b + j + 1].to_broadcast([P, P]), ident[:])
-                copy(pool[:].rearrange("p (n j) -> p n j", j=8)[:, :, 4 * b : 4 * b + 4], bank[:].rearrange("p j n -> p n j"))
-
-        spread(pos_cols, pos_pool, lambda o, i: nc.vector.tensor_copy(out=o, in_=i), "spread_a")
         k_words = held.tile([P, N, 2], U32, name="k_words", align_bytes=64)
         pair_up("scalar", k_pairs[0], k_raw[0], 0, 512)
         pair_up("vector", k_pairs[0], k_raw[0], 512, 1024)
         nc.vector.tensor_copy(k_words[:, :, 0], k_pairs[0][:].bitcast(U32).indirect(offsets[:]))
-        spread(vs_cols, vs_pool, lambda o, i: nc.scalar.activation(o, i, COPY), "spread_b")
         pos_listed = held.tile([P, N], F32, name="pos_listed")
         nc.vector.tensor_copy(pos_listed[:], pos_pool[:].indirect(offsets[:]))
-        vs_listed = held.tile([P, N], F32, name="vs_listed")
-        nc.vector.tensor_copy(vs_listed[:], vs_pool[:].indirect(offsets[:]))
         pair_up("scalar", k_pairs[1], k_raw[1], 0, 512)
-        pair_up("scalar", k_pairs[1], k_raw[1], 512, 688)
-        pair_up("vector", k_pairs[1], k_raw[1], 688, 1024)
+        pair_up("scalar", k_pairs[1], k_raw[1], 512, 624)
+        pair_up("vector", k_pairs[1], k_raw[1], 624, 1024)
         nc.vector.tensor_copy(k_words[:, :, 1], k_pairs[1][:].bitcast(U32).indirect(offsets[:]))
         q_grouped = held.tile([P, NQ, 4], BF16, name="q_grouped", align_bytes=64)
         nc.scalar.activation(q_grouped[:], q_raw[:].rearrange("p t q -> p q t"), COPY)
@@ -112,8 +99,8 @@ def tile_attend_ring_alibi_kernel(tc, qT, kT, vT, vs, pos, slope, offs, out):
             nc.tensor.matmul_mx(out=bank[:], lhsT=q_codes[:].bitcast(FP8X4), lhsT_scale=q_scales[:], rhs=k_codes[:, cols].bitcast(FP8X4), rhs_scale=k_scales[:, cols], start=True, stop=True)
             scores.append(bank)
 
-        pair_up("scalar", v_pairs, v_raw, 0, 512)
-        pair_up("scalar", v_pairs, v_raw, 512, 768)
+        for h in range(2):
+            nc.scalar.activation(v_pairs[:, h * T : (h + 1) * T].rearrange("p (n t) -> p n t", t=2), v_raw[h][:].rearrange("p t n -> p n t"), COPY)
         s = held.tile([P, N], F32, name="s")
         for h in range(2):
             cols = slice(h * H, (h + 1) * H)
@@ -121,27 +108,27 @@ def tile_attend_ring_alibi_kernel(tc, qT, kT, vT, vs, pos, slope, offs, out):
         minus_m = held.tile([P, 1], F32, name="minus_m")
         nc.vector.tensor_reduce(out=minus_m[:], in_=s[:], axis=X, op=MAX, negate=True)
 
-        pair_up("vector", v_pairs, v_raw, 768, 1024)
         s4 = s[:].rearrange("p (i u e) -> p i u e", u=2, e=2)
         pr, sums = [], []
         for u in range(2):
-            pu = held.tile([P, N // 4, 2], F32, name=f"p{u}")
+            pu = held.tile([P, N // 4, 2], F32, name=f"p{u}", tag=f"v_raw{1 - u}")
             su = held.tile([P, 1], F32, name=f"sum{u}")
             nc.scalar.activation(pu[:], s4[:, :, u, :], EXP, bias=minus_m[:], accum_out=su[:])
             pr.append(pu)
             sums.append(su)
 
-        v_words = held.tile([P, N], U32, name="v_words", align_bytes=64)
-        nc.vector.tensor_copy(v_words[:], v_pairs[:].bitcast(U32).indirect(offsets[:]))
+        v_words = held.tile([P, 4, N // 4], U32, name="v_words", align_bytes=64)
+        nc.vector.tensor_copy(v_words[:].rearrange("p t i -> p i t"), v_pairs[:].bitcast(U32).indirect(offsets[:]))
         v_bank = psum.tile([P, 4, P], F32, name="v_bank")
-        v_f32 = v_words[:].bitcast(F32)
         for t in range(4):
-            nc.tensor.transpose(v_bank[:, t, :], v_f32[:, t : N : 4], ident[:])
+            nc.tensor.transpose(v_bank[:, t, :], v_words[:, t, :].bitcast(F32), ident[:])
         v_grouped = held.tile([P, DV, 4], BF16, name="v_grouped", align_bytes=64)
         v_turned = v_bank[:].rearrange("p t w -> p (t w)").bitcast(BF16).rearrange("p (t e) -> p e t", t=4)
         nc.scalar.copy(v_grouped[:], v_turned)
         v_codes, v_scales = quantise("v", None, DV)
 
+        vs_listed = held.tile([P, N], F32, name="vs_listed", tag="v_pairs", align_bytes=64)
+        nc.vector.tensor_copy(vs_listed[:], vs_pool[:].indirect(offsets[:]))
         vs4 = vs_listed[:].rearrange("p (i u e) -> p i u e", u=2, e=2)
         w_bank = psum.tile([P, 2, P], F32, name="w_bank")
         for u in range(2):
@@ -150,7 +137,7 @@ def tile_attend_ring_alibi_kernel(tc, qT, kT, vT, vs, pos, slope, offs, out):
             nc.tensor.transpose(w_bank[:, u, :], wu[:].rearrange("p i e -> p (i e)").bitcast(F32), ident[:])
         w_grouped = held.tile([P, NQ, 4], BF16, name="w_grouped", align_bytes=64)
         w_words = w_grouped[:].rearrange("p q t -> p (q t)").bitcast(F32).rearrange("p (q u) -> p q u", u=2)
-        nc.scalar.copy(w_words, w_bank[:].rearrange("p u q -> p q u"))
+        nc.vector.tensor_copy(out=w_words, in_=w_bank[:].rearrange("p u q -> p q u"))
         total = held.tile([P, 1], F32, name="total")
         nc.vector.tensor_tensor(total[:], sums[0][:], sums[1][:], ADD)
         inv = held.tile([P, 1], F32, name="inv")
@@ -162,7 +149,7 @@ def tile_attend_ring_alibi_kernel(tc, qT, kT, vT, vs, pos, slope, offs, out):
         HV = DV // 2
         for h in range(2):
             cols = slice(h * HV, (h + 1) * HV)
-            y = psum.tile([P, HV], F32, name=f"y{h}", tag=f"spread_a{h}")
+            y = psum.tile([P, HV], F32, name=f"y{h}")
             nc.tensor.matmul_mx(out=y[:], lhsT=w_codes[:].bitcast(FP8X4), lhsT_scale=w_scales[:], rhs=v_codes[:, cols].bitcast(FP8X4), rhs_scale=v_scales[:, cols], start=True, stop=True)
             res = held.tile([P, HV], F32, name=f"res{h}")
             if h == 0:

@@ -28,7 +28,8 @@ def tile_attend_ring_alibi_kernel(tc, qT, kT, vT, vs, pos, slope, offs, out):
         offsets = held.tile([P, N // 16], U16, name="offsets")
         k_raw = [held.tile([P, 2, T], F32, name=f"k_raw{u}") for u in range(2)]
         k_pairs = [held.tile([P, 2 * T], BF16, name=f"k_pairs{u}", align_bytes=64) for u in range(2)]
-        v_raw = [held.tile([P, 2, T // 2], F32, name=f"v_raw{h}", tag=f"v_raw{h}") for h in range(2)]
+        v_parts = [(0, 640), (640, T)]
+        v_raw = [held.tile([P, 2, b - a], F32, name=f"v_raw{h}", tag=f"v_raw{h}") for h, (a, b) in enumerate(v_parts)]
         v_pairs = held.tile([P, 2 * T], BF16, name="v_pairs", tag="v_pairs", align_bytes=64)
         q_raw = held.tile([P, 4, NQ], F32, name="q_raw")
         pos_pool = held.tile([P, T], F32, name="pos_pool")
@@ -42,16 +43,18 @@ def tile_attend_ring_alibi_kernel(tc, qT, kT, vT, vs, pos, slope, offs, out):
             cols = slice(h * (T // parts), (h + 1) * (T // parts))
             nc.sync.dma_start(out=tile[:, :, cols], in_=rows[:, :, cols])
 
+        slope_rows = held.tile([P, P], F32, name="slope_rows")
+        nc.gpsimd.memset(slope_rows[:], 0.0)
         load_half(k_raw[0], k_rows[:, 0:2, :], 0)
         nc.sync.dma_start(offsets[:], offs)
+        nc.sync.dma_start(out=slope_rows[0:1, :], in_=slope[0].rearrange("q o -> o q"))
         load_half(k_raw[0], k_rows[:, 0:2, :], 1)
-        nc.sync.dma_start(out=pos_pool[:], in_=pos)
         load_half(k_raw[1], k_rows[:, 2:4, :], 0)
         load_half(k_raw[1], k_rows[:, 2:4, :], 1)
         nc.sync.dma_start(out=q_raw[:], in_=qT[0].rearrange("(p t) q -> p t q", t=4))
-        nc.sync.dma_start(out=slope_col[:], in_=slope[0])
-        for h in range(2):
-            nc.sync.dma_start(out=v_raw[h][:], in_=v_rows[:, :, h * (T // 2) : (h + 1) * (T // 2)])
+        nc.sync.dma_start(out=pos_pool[:], in_=pos)
+        for h, (a, b) in enumerate(v_parts):
+            nc.sync.dma_start(out=v_raw[h][:], in_=v_rows[:, :, a:b])
         nc.sync.dma_start(out=vs_pool[:], in_=vs)
 
         warm = held.tile([P, 1], F32, name="warm")
@@ -77,9 +80,10 @@ def tile_attend_ring_alibi_kernel(tc, qT, kT, vT, vs, pos, slope, offs, out):
         k_words = held.tile([P, N, 2], U32, name="k_words", align_bytes=64)
         pair_up("scalar", k_pairs[0], k_raw[0], 0, 512)
         pair_up("vector", k_pairs[0], k_raw[0], 512, 1024)
+        slope_bank = psum.tile([P, P], F32, name="slope_bank")
+        nc.tensor.transpose(slope_bank[:], slope_rows[:], ident[:])
+        nc.scalar.copy(slope_col[:], slope_bank[:, 0:1])
         nc.vector.tensor_copy(k_words[:, :, 0], k_pairs[0][:].bitcast(U32).indirect(offsets[:]))
-        pos_listed = held.tile([P, N], F32, name="pos_listed")
-        nc.vector.tensor_copy(pos_listed[:], pos_pool[:].indirect(offsets[:]))
         pair_up("scalar", k_pairs[1], k_raw[1], 0, 512)
         pair_up("scalar", k_pairs[1], k_raw[1], 512, 624)
         pair_up("vector", k_pairs[1], k_raw[1], 624, 1024)
@@ -99,19 +103,22 @@ def tile_attend_ring_alibi_kernel(tc, qT, kT, vT, vs, pos, slope, offs, out):
             nc.tensor.matmul_mx(out=bank[:], lhsT=q_codes[:].bitcast(FP8X4), lhsT_scale=q_scales[:], rhs=k_codes[:, cols].bitcast(FP8X4), rhs_scale=k_scales[:, cols], start=True, stop=True)
             scores.append(bank)
 
-        for h in range(2):
-            nc.scalar.activation(v_pairs[:, h * T : (h + 1) * T].rearrange("p (n t) -> p n t", t=2), v_raw[h][:].rearrange("p t n -> p n t"), COPY)
+        v_dst = [v_pairs[:, 2 * a : 2 * b].rearrange("p (n t) -> p n t", t=2) for a, b in v_parts]
+        nc.scalar.activation(v_dst[0], v_raw[0][:].rearrange("p t n -> p n t"), COPY)
+        pos_listed = held.tile([P, N], F32, name="pos_listed")
+        nc.vector.tensor_copy(pos_listed[:], pos_pool[:].indirect(offsets[:]))
         s = held.tile([P, N], F32, name="s")
         for h in range(2):
             cols = slice(h * H, (h + 1) * H)
             nc.vector.scalar_tensor_tensor(out=s[:, cols], in0=pos_listed[:, cols], scalar=slope_col[:], in1=scores[h][:], op0=MULT, op1=ADD)
-        minus_m = held.tile([P, 1], F32, name="minus_m")
+        nc.vector.tensor_copy(out=v_dst[1], in_=v_raw[1][:].rearrange("p t n -> p n t"))
+        minus_m = held.tile([P, 1], F32, name="minus_m", tag="v_raw1")
         nc.vector.tensor_reduce(out=minus_m[:], in_=s[:], axis=X, op=MAX, negate=True)
 
         s4 = s[:].rearrange("p (i u e) -> p i u e", u=2, e=2)
         pr, sums = [], []
         for u in range(2):
-            pu = held.tile([P, N // 4, 2], F32, name=f"p{u}", tag=f"v_raw{1 - u}")
+            pu = held.tile([P, N // 4, 2], F32, name=f"p{u}", tag="v_raw0" if u == 0 else "p1")
             su = held.tile([P, 1], F32, name=f"sum{u}")
             nc.scalar.activation(pu[:], s4[:, :, u, :], EXP, bias=minus_m[:], accum_out=su[:])
             pr.append(pu)
@@ -124,7 +131,7 @@ def tile_attend_ring_alibi_kernel(tc, qT, kT, vT, vs, pos, slope, offs, out):
             nc.tensor.transpose(v_bank[:, t, :], v_words[:, t, :].bitcast(F32), ident[:])
         v_grouped = held.tile([P, DV, 4], BF16, name="v_grouped", align_bytes=64)
         v_turned = v_bank[:].rearrange("p t w -> p (t w)").bitcast(BF16).rearrange("p (t e) -> p e t", t=4)
-        nc.scalar.copy(v_grouped[:], v_turned)
+        nc.scalar.copy(v_grouped[:, 0:P, :], v_turned[:, 0:P, :])
         v_codes, v_scales = quantise("v", None, DV)
 
         vs_listed = held.tile([P, N], F32, name="vs_listed", tag="v_pairs", align_bytes=64)
@@ -135,14 +142,16 @@ def tile_attend_ring_alibi_kernel(tc, qT, kT, vT, vs, pos, slope, offs, out):
             wu = held.tile([P, N // 4, 2], BF16, name=f"w{u}", align_bytes=64)
             nc.vector.tensor_tensor(wu[:], pr[u][:], vs4[:, :, u, :], MULT)
             nc.tensor.transpose(w_bank[:, u, :], wu[:].rearrange("p i e -> p (i e)").bitcast(F32), ident[:])
-        w_grouped = held.tile([P, NQ, 4], BF16, name="w_grouped", align_bytes=64)
-        w_words = w_grouped[:].rearrange("p q t -> p (q t)").bitcast(F32).rearrange("p (q u) -> p q u", u=2)
-        nc.vector.tensor_copy(out=w_words, in_=w_bank[:].rearrange("p u q -> p q u"))
         total = held.tile([P, 1], F32, name="total")
         nc.vector.tensor_tensor(total[:], sums[0][:], sums[1][:], ADD)
         inv = held.tile([P, 1], F32, name="inv")
         nc.vector.reciprocal(inv[:], total[:])
-        nc.vector.quantize_mx(out=v_codes[:].bitcast(FP8X4), scales=v_scales[:], in_=v_grouped[:].rearrange("p e t -> p (e t)"))
+        nc.vector.tensor_copy(out=v_grouped[:, P:DV, :], in_=v_turned[:, P:DV, :])
+        nc.vector.quantize_mx(out=v_codes[:, 0:128].bitcast(FP8X4), scales=v_scales[:, 0:128], in_=v_grouped[:, 0:128, :].rearrange("p e t -> p (e t)"))
+        nc.vector.quantize_mx(out=v_codes[:, 128:256].bitcast(FP8X4), scales=v_scales[:, 128:256], in_=v_grouped[:, 128:256, :].rearrange("p e t -> p (e t)"))
+        w_grouped = held.tile([P, NQ, 4], BF16, name="w_grouped", align_bytes=64)
+        w_words = w_grouped[:].rearrange("p q t -> p (q t)").bitcast(F32).rearrange("p (q u) -> p q u", u=2)
+        nc.scalar.copy(w_words, w_bank[:].rearrange("p u q -> p q u"))
         w_codes, w_scales = quantise("w", None, NQ)
         nc.vector.quantize_mx(out=w_codes[:].bitcast(FP8X4), scales=w_scales[:], in_=w_grouped[:].rearrange("p q t -> p (q t)"))
 

from contextlib import ExitStack

import concourse.mybir as mybir
from concourse.masks import make_identity

NQ, D, N, T, DV = 128, 512, 512, 1024, 256
P = 128
FLOPS = 2 * NQ * N * (D + DV)

F32 = mybir.dt.float32
BF16 = mybir.dt.bfloat16
U32 = mybir.dt.uint32
U16 = mybir.dt.uint16
U8 = mybir.dt.uint8
FP8X4 = mybir.dt.float8_e4m3fn_x4
ADD, MULT, MAX = mybir.AluOpType.add, mybir.AluOpType.mult, mybir.AluOpType.max
EXP = mybir.ActivationFunctionType.Exp
COPY = mybir.ActivationFunctionType.Copy
X = mybir.AxisListType.X


def tile_attend_ring_alibi_kernel(tc, qT, kT, vT, vs, pos, slope, offs, out):
    nc = tc.nc
    with ExitStack() as ctx:
        held = ctx.enter_context(tc.tile_pool(name="held", bufs=1))
        psum = ctx.enter_context(tc.psum_pool(name="psum", bufs=1))

        offsets = held.tile([P, N // 16], U16, name="offsets")
        k_raw = [held.tile([P, 2, T], F32, name=f"k_raw{u}") for u in range(2)]
        k_pairs = [held.tile([P, 2 * T], BF16, name=f"k_pairs{u}", align_bytes=64) for u in range(2)]
        v_parts = [(0, 640), (640, T)]
        v_raw = [held.tile([P, 2, b - a], F32, name=f"v_raw{h}", tag=f"v_raw{h}") for h, (a, b) in enumerate(v_parts)]
        v_pairs = held.tile([P, 2 * T], BF16, name="v_pairs", tag="v_pairs", align_bytes=64)
        q_raw = held.tile([P, 4, NQ], F32, name="q_raw")
        pos_pool = held.tile([P, T], F32, name="pos_pool")
        vs_pool = held.tile([P, T], F32, name="vs_pool")
        slope_col = held.tile([P, 1], F32, name="slope_col")

        k_rows = kT.rearrange("(p t) n -> p t n", t=4)
        v_rows = vT.rearrange("(p t) n -> p t n", t=2)

        def load_half(tile, rows, h, parts=2):
            cols = slice(h * (T // parts), (h + 1) * (T // parts))
            nc.sync.dma_start(out=tile[:, :, cols], in_=rows[:, :, cols])

        slope_rows = held.tile([P, P], F32, name="slope_rows")
        nc.gpsimd.memset(slope_rows[:], 0.0)
        load_half(k_raw[0], k_rows[:, 0:2, :], 0)
        nc.sync.dma_start(offsets[:], offs)
        nc.sync.dma_start(out=slope_rows[0:1, :], in_=slope[0].rearrange("q o -> o q"))
        load_half(k_raw[0], k_rows[:, 0:2, :], 1)
        load_half(k_raw[1], k_rows[:, 2:4, :], 0)
        load_half(k_raw[1], k_rows[:, 2:4, :], 1)
        nc.sync.dma_start(out=q_raw[:], in_=qT[0].rearrange("(p t) q -> p t q", t=4))
        nc.sync.dma_start(out=pos_pool[:], in_=pos)
        for h, (a, b) in enumerate(v_parts):
            nc.sync.dma_start(out=v_raw[h][:], in_=v_rows[:, :, a:b])
        nc.sync.dma_start(out=vs_pool[:], in_=vs)

        warm = held.tile([P, 1], F32, name="warm")
        warm_out = held.tile([P, 1], F32, name="warm_out")
        nc.vector.memset(warm[:], 0.0)
        nc.scalar.activation(warm_out[:], warm[:], EXP)
        ident = held.tile([P, P], F32, name="ident")
        make_identity(nc, ident[:])

        def pair_up(engine, pairs, raw, a, b):
            dst = pairs[:, 2 * a : 2 * b].rearrange("p (n t) -> p n t", t=2)
            src = raw[:, :, a:b].rearrange("p t n -> p n t")
            if engine == "scalar":
                nc.scalar.activation(dst, src, COPY)
            else:
                nc.vector.tensor_copy(out=dst, in_=src)

        def quantise(name, src, width):
            codes = held.tile([P, width], U32, name=name + "_codes", align_bytes=64)
            scales = held.tile([P, width], U8, name=name + "_scales", align_bytes=64)
            return codes, scales

        k_words = held.tile([P, N, 2], U32, name="k_words", align_bytes=64)
        pair_up("scalar", k_pairs[0], k_raw[0], 0, 512)
        pair_up("vector", k_pairs[0], k_raw[0], 512, 1024)
        slope_bank = psum.tile([P, P], F32, name="slope_bank")
        nc.tensor.transpose(slope_bank[:], slope_rows[:], ident[:])
        nc.scalar.copy(slope_col[:], slope_bank[:, 0:1])
        nc.vector.tensor_copy(k_words[:, :, 0], k_pairs[0][:].bitcast(U32).indirect(offsets[:]))
        pair_up("scalar", k_pairs[1], k_raw[1], 0, 512)
        pair_up("scalar", k_pairs[1], k_raw[1], 512, 624)
        pair_up("vector", k_pairs[1], k_raw[1], 624, 1024)
        nc.vector.tensor_copy(k_words[:, :, 1], k_pairs[1][:].bitcast(U32).indirect(offsets[:]))
        q_grouped = held.tile([P, NQ, 4], BF16, name="q_grouped", align_bytes=64)
        nc.scalar.activation(q_grouped[:], q_raw[:].rearrange("p t q -> p q t"), COPY)
        q_codes, q_scales = quantise("q", None, NQ)
        nc.vector.quantize_mx(out=q_codes[:].bitcast(FP8X4), scales=q_scales[:], in_=q_grouped[:].rearrange("p q t -> p (q t)"))
        k_codes, k_scales = quantise("k", None, N)
        k_flat = k_words[:].rearrange("p n u -> p (n u)").bitcast(BF16)
        H = N // 2
        scores = []
        for h in range(2):
            cols = slice(h * H, (h + 1) * H)
            nc.vector.quantize_mx(out=k_codes[:, cols].bitcast(FP8X4), scales=k_scales[:, cols], in_=k_flat[:, 4 * h * H : 4 * (h + 1) * H])
            bank = psum.tile([P, H], F32, name=f"scores{h}")
            nc.tensor.matmul_mx(out=bank[:], lhsT=q_codes[:].bitcast(FP8X4), lhsT_scale=q_scales[:], rhs=k_codes[:, cols].bitcast(FP8X4), rhs_scale=k_scales[:, cols], start=True, stop=True)
            scores.append(bank)

        v_dst = [v_pairs[:, 2 * a : 2 * b].rearrange("p (n t) -> p n t", t=2) for a, b in v_parts]
        nc.scalar.activation(v_dst[0], v_raw[0][:].rearrange("p t n -> p n t"), COPY)
        pos_listed = held.tile([P, N], F32, name="pos_listed")
        nc.vector.tensor_copy(pos_listed[:], pos_pool[:].indirect(offsets[:]))
        s = held.tile([P, N], F32, name="s")
        for h in range(2):
            cols = slice(h * H, (h + 1) * H)
            nc.vector.scalar_tensor_tensor(out=s[:, cols], in0=pos_listed[:, cols], scalar=slope_col[:], in1=scores[h][:], op0=MULT, op1=ADD)
        nc.vector.tensor_copy(out=v_dst[1], in_=v_raw[1][:].rearrange("p t n -> p n t"))
        minus_m = held.tile([P, 1], F32, name="minus_m", tag="v_raw1")
        nc.vector.tensor_reduce(out=minus_m[:], in_=s[:], axis=X, op=MAX, negate=True)

        s4 = s[:].rearrange("p (i u e) -> p i u e", u=2, e=2)
        pr, sums = [], []
        for u in range(2):
            pu = held.tile([P, N // 4, 2], F32, name=f"p{u}", tag="v_raw0" if u == 0 else "p1")
            su = held.tile([P, 1], F32, name=f"sum{u}")
            nc.scalar.activation(pu[:], s4[:, :, u, :], EXP, bias=minus_m[:], accum_out=su[:])
            pr.append(pu)
            sums.append(su)

        v_words = held.tile([P, 4, N // 4], U32, name="v_words", align_bytes=64)
        nc.vector.tensor_copy(v_words[:].rearrange("p t i -> p i t"), v_pairs[:].bitcast(U32).indirect(offsets[:]))
        v_bank = psum.tile([P, 4, P], F32, name="v_bank")
        for t in range(4):
            nc.tensor.transpose(v_bank[:, t, :], v_words[:, t, :].bitcast(F32), ident[:])
        v_grouped = held.tile([P, DV, 4], BF16, name="v_grouped", align_bytes=64)
        v_turned = v_bank[:].rearrange("p t w -> p (t w)").bitcast(BF16).rearrange("p (t e) -> p e t", t=4)
        nc.scalar.copy(v_grouped[:, 0:P, :], v_turned[:, 0:P, :])
        v_codes, v_scales = quantise("v", None, DV)

        vs_listed = held.tile([P, N], F32, name="vs_listed", tag="v_pairs", align_bytes=64)
        nc.vector.tensor_copy(vs_listed[:], vs_pool[:].indirect(offsets[:]))
        vs4 = vs_listed[:].rearrange("p (i u e) -> p i u e", u=2, e=2)
        w_bank = psum.tile([P, 2, P], F32, name="w_bank")
        for u in range(2):
            wu = held.tile([P, N // 4, 2], BF16, name=f"w{u}", align_bytes=64)
            nc.vector.tensor_tensor(wu[:], pr[u][:], vs4[:, :, u, :], MULT)
            nc.tensor.transpose(w_bank[:, u, :], wu[:].rearrange("p i e -> p (i e)").bitcast(F32), ident[:])
        total = held.tile([P, 1], F32, name="total")
        nc.vector.tensor_tensor(total[:], sums[0][:], sums[1][:], ADD)
        inv = held.tile([P, 1], F32, name="inv")
        nc.vector.reciprocal(inv[:], total[:])
        nc.vector.tensor_copy(out=v_grouped[:, P:DV, :], in_=v_turned[:, P:DV, :])
        nc.vector.quantize_mx(out=v_codes[:, 0:128].bitcast(FP8X4), scales=v_scales[:, 0:128], in_=v_grouped[:, 0:128, :].rearrange("p e t -> p (e t)"))
        nc.vector.quantize_mx(out=v_codes[:, 128:256].bitcast(FP8X4), scales=v_scales[:, 128:256], in_=v_grouped[:, 128:256, :].rearrange("p e t -> p (e t)"))
        w_grouped = held.tile([P, NQ, 4], BF16, name="w_grouped", align_bytes=64)
        w_words = w_grouped[:].rearrange("p q t -> p (q t)").bitcast(F32).rearrange("p (q u) -> p q u", u=2)
        nc.scalar.copy(w_words, w_bank[:].rearrange("p u q -> p q u"))
        w_codes, w_scales = quantise("w", None, NQ)
        nc.vector.quantize_mx(out=w_codes[:].bitcast(FP8X4), scales=w_scales[:], in_=w_grouped[:].rearrange("p q t -> p (q t)"))

        HV = DV // 2
        for h in range(2):
            cols = slice(h * HV, (h + 1) * HV)
            y = psum.tile([P, HV], F32, name=f"y{h}")
            nc.tensor.matmul_mx(out=y[:], lhsT=w_codes[:].bitcast(FP8X4), lhsT_scale=w_scales[:], rhs=v_codes[:, cols].bitcast(FP8X4), rhs_scale=v_scales[:, cols], start=True, stop=True)
            res = held.tile([P, HV], F32, name=f"res{h}")
            if h == 0:
                nc.scalar.activation(res[:], y[:], COPY, scale=inv[:])
            else:
                nc.vector.tensor_scalar(res[:], y[:], inv[:], None, MULT)
            nc.sync.dma_start(out=out[0][:, cols], in_=res[:])
